import numpy as np, ml_dtypes
CORES = [89,94,345,350]
N = 4
TK = 32
def setup_inputs(rng):
    x = rng.standard_normal((N, 128, TK), dtype=np.float32).astype(ml_dtypes.bfloat16); w1 = (rng.standard_normal((N, 128, 128), dtype=np.float32) / 8).astype(ml_dtypes.bfloat16)
    wa = np.concatenate(list(w1.astype(np.float64)), axis=1)
    for r in range(N):
        while True:
            near = (np.abs(wa.T @ x[r].astype(np.float64)) < 2e-4).any(axis=0)
            if not near.any(): break
            x[r][:, near] = rng.standard_normal((128, int(near.sum())), dtype=np.float32).astype(ml_dtypes.bfloat16)
    return {"x": x, "dy": rng.standard_normal((N, 128, TK), dtype=np.float32).astype(ml_dtypes.bfloat16), "w1": w1, "w2t": (rng.standard_normal((N, 128, 128), dtype=np.float32) / 8).astype(ml_dtypes.bfloat16)}
def setup_inputs_big(rng):
    d = setup_inputs(rng)
    for k in ("x", "dy", "w1", "w2t"): d[k] = (d[k].astype(np.float32) * 1024.0).astype(d[k].dtype)
    return d
def setup_inputs_small(rng):
    d = setup_inputs(rng)
    for k in ("x", "dy", "w1", "w2t"): d[k] = (d[k].astype(np.float32) * (1 / 1024.0)).astype(d[k].dtype)
    return d
def setup_inputs_apart(rng):
    d = setup_inputs(rng)
    f = (10.0 ** rng.permutation(np.linspace(-1.5, 1.5, N))).astype(np.float32).reshape(N, 1, 1)
    for k in ("x", "dy", "w1", "w2t"): d[k] = (d[k].astype(np.float32) * f).astype(d[k].dtype)
    return d
def reference(x, dy, w1, w2t):
    X, DY, W1, W2T = x.astype(np.float64), dy.astype(np.float64), w1.astype(np.float64), w2t.astype(np.float64)
    dx = np.zeros((N, 128, TK))
    for r in range(N):
        for j in range(N):
            dx[r] += W1[j] @ ((W1[j].T @ X[r] > 0) * (W2T[j].T @ DY[r]))
    return {"dx": dx.astype(ml_dtypes.bfloat16)}

@@ -1,0 +1,159 @@
+from concourse.bass import DstId, RemoteDMATransfer
+from concourse.mybir import AluOpType
+
+TK = 32
+D = 128
+NHOSTS = 4
+
+SCRATCH = {
+    "wbuf": ("sbuf", [128, 2 * D], "bfloat16"),
+    "tbuf": ("sbuf", [128, 2, TK], "bfloat16"),
+    "lw": ("sbuf", [128, 2, 2 * D], "bfloat16"),
+    "lt": ("sbuf", [128, 2, 2, TK], "bfloat16"),
+    "part": ("sbuf", [128, TK], "bfloat16"),
+    "ident": ("sbuf", [128, D], "bfloat16"),
+    "w1t": ("sbuf", [128, 2, D], "bfloat16"),
+    "mb": ("sbuf", [128, 2, 2 * TK], "bfloat16"),
+    "gb": ("sbuf", [128, 2, 2 * TK], "bfloat16"),
+    "outb": ("sbuf", [128, 2 * TK], "bfloat16"),
+    "pz0": ("psum", [128, 512], "float32"), "pz1": ("psum", [128, 512], "float32"),
+    "pu0": ("psum", [128, 512], "float32"), "pu1": ("psum", [128, 512], "float32"),
+    "pt0": ("psum", [128, 1024], "bfloat16"), "pt1": ("psum", [128, 1024], "bfloat16"),
+    "pacc": ("psum", [128, 512], "float32"),
+}
+SEMAPHORES = ["ldw", "ldt", "ones", "idn", "wa0", "wa1", "tok", "sent", "pin", "tp0", "tp1", "tc0", "tc1",
+              "z0", "z1", "u0", "u1", "m0", "m1", "g0", "g1", "acc", "outr", "st"]
+
+
+def _engines(mask, n, skip=0):
+    bits = [b for b in range(mask.bit_length()) if (mask >> b) & 1][skip:skip + n]
+    return sum(1 << b for b in bits)
+
+
+def _count(mask):
+    return sum((mask >> b) & 1 for b in range(mask.bit_length()))
+
+
+def _plan(T, topo):
+    ranks = list(T.cores)
+    hosts = sorted({topo.host(c) for c in ranks})
+    by = {h: [c for c in ranks if topo.host(c) == h] for h in hosts}
+    meet = {}
+    for ht in hosts:
+        for m in range(NHOSTS):
+            if m in hosts or topo.rack(m) != topo.rack(ht):
+                continue
+            mc = by[ht][0] + (m - ht) * topo.CORES_PER_HOST
+            if all(topo.may_write(c, mc) for c in ranks) and all(topo.may_write(mc, c) for c in by[ht]):
+                meet[ht] = mc
+    return hosts, by, meet
+
+
+def _identity(g, T):
+    S = T.sem
+    g.vector.memset(T.ident[:], 1.0).then_inc(S.ones, 1)
+    g.wait_ge(S.ones, 1)
+    g.affine_select(T.ident[:], T.ident[:], [[-1, D]], AluOpType.is_equal, 0.0, 0, 1).then_inc(S.idn, 1)
+
+
+def _compute(g, T, W, wready, X, DY, tready, n):
+    S = T.sem
+    pe, ve = g.tensor, g.vector
+    pz, pu, pt = [T.pz0, T.pz1], [T.pu0, T.pu1], [T.pt0, T.pt1]
+    pe.wait_ge(S.idn, 1)
+    for j in range(2):
+        pe.wait_ge(*wready[j])
+        pe.transpose(pt[j][:, 0:D], W[j][0], T.ident[:]).then_inc(S["tp%d" % j], 1)
+    pe.wait_ge(*tready)
+    for j in range(2):
+        pe.matmul(pz[j][:, 0:n], W[j][0], X, True, True).then_inc(S["z%d" % j], 1)
+        pe.matmul(pu[j][:, 0:n], W[j][1], DY, True, True).then_inc(S["u%d" % j], 1)
+    for j in range(2):
+        pe.wait_ge(S["tc%d" % j], 1)
+        pe.wait_ge(S["g%d" % j], 1)
+        mm = pe.matmul(T.pacc[:, 0:n], T.w1t[:, j, :], T.gb[:, j, 0:n], j == 0, j == 1)
+    mm.then_inc(S.acc, 1)
+    for j in range(2):
+        ve.wait_ge(S["tp%d" % j], 1)
+        ve.tensor_copy(T.w1t[:, j, :], pt[j][:, 0:D]).then_inc(S["tc%d" % j], 1)
+    for j in range(2):
+        ve.wait_ge(S["z%d" % j], 1)
+        ve.tensor_scalar(T.mb[:, j, 0:n], pz[j][:, 0:n], 0.0, None, AluOpType.is_gt).then_inc(S["m%d" % j], 1)
+        ve.wait_ge(S["u%d" % j], 1)
+        ve.wait_ge(S["m%d" % j], 1)
+        ve.tensor_tensor(T.gb[:, j, 0:n], T.mb[:, j, 0:n], pu[j][:, 0:n], AluOpType.mult).then_inc(S["g%d" % j], 1)
+    ve.wait_ge(S.acc, 1)
+
+
+def _rank(g, core, T, topo, hosts, by, meet):
+    S = T.sem
+    h = topo.host(core)
+    other = [x for x in hosts if x != h][0]
+    slot = by[h].index(core)
+    peer = [c for c in by[h] if c != core][0]
+    far, near = meet[other], meet[h]
+    g.sync.dma_start(T.wbuf[:, 0:D], T.w1[:]).then_inc(S.ldw, 16)
+    g.scalar.dma_start(T.wbuf[:, D:2 * D], T.w2t[:]).then_inc(S.ldw, 16)
+    g.sync.dma_start(T.tbuf[:, 0, :], T.x[:]).then_inc(S.ldt, 16)
+    g.scalar.dma_start(T.tbuf[:, 1, :], T.dy[:]).then_inc(S.ldt, 16)
+    _identity(g, T)
+    sent = 0
+    mk = topo.mask(core, far)
+    rid, pid = topo.addr(far, core)
+    g.wait_ge(S.ldw, 32)
+    g.remote_dma(out_ap=T.lw[:, slot, :], in_ap=T.wbuf[:], remote_sem=S["wa%d" % slot], local_sem=S.sent,
+                 pid=pid, routing_id=rid, dma_engine_mask=mk)
+    sent += _count(mk)
+    mk = topo.mask(core, near)
+    rid, pid = topo.addr(near, core)
+    g.wait_ge(S.ldt, 32)
+    g.remote_dma(out_ap=T.lt[:, slot], in_ap=T.tbuf[:], remote_sem=S.tok, local_sem=S.sent,
+                 pid=pid, routing_id=rid, dma_engine_mask=mk)
+    sent += _count(mk)
+    mk = topo.mask(core, peer) & ~topo.mask(core, far)
+    rid, pid = topo.addr(peer, core)
+    g.remote_dma(out_ap=T.lw[:, 0, :], in_ap=T.wbuf[:], remote_sem=S.wa0, local_sem=S.sent,
+                 pid=pid, routing_id=rid, dma_engine_mask=mk)
+    npeer = _count(mk)
+    sent += npeer
+    _compute(g, T, [(T.wbuf[:, 0:D], T.wbuf[:, D:2 * D]), (T.lw[:, 0, 0:D], T.lw[:, 0, D:2 * D])],
+             [(S.ldw, 32), (S.wa0, npeer)], T.tbuf[:, 0, :], T.tbuf[:, 1, :], (S.ldt, 32), TK)
+    nback = _count(topo.mask(near, core)) // len(by[h])
+    g.vector.wait_ge(S.pin, nback)
+    g.vector.tensor_tensor(T.outb[:, 0:TK], T.pacc[:, 0:TK], T.part[:], AluOpType.add).then_inc(S.outr, 1)
+    g.sync.wait_ge(S.outr, 1)
+    g.sync.dma_start(T.dx[:], T.outb[:, 0:TK]).then_inc(S.st, 16)
+    g.sync.wait_ge(S.st, 16)
+    g.wait_ge(S.sent, sent)
+
+
+def _meeting(g, core, T, topo, toks, wts):
+    S = T.sem
+    _identity(g, T)
+    n = len(toks) * TK
+    nw = [_count(topo.mask(c, core)) for c in wts]
+    nt = sum(_count(topo.mask(c, core)) for c in toks)
+    _compute(g, T, [(T.lw[:, j, 0:D], T.lw[:, j, D:2 * D]) for j in range(2)], [(S.wa0, nw[0]), (S.wa1, nw[1])],
+             T.lt[:, :, 0, :], T.lt[:, :, 1, :], (S.tok, nt), n)
+    g.vector.tensor_copy(T.outb[:, 0:n], T.pacc[:, 0:n]).then_inc(S.outr, 1)
+    g.wait_ge(S.outr, 1)
+    trs, sent = [], 0
+    for i, c in enumerate(toks):
+        full = topo.mask(core, c)
+        k = _count(full) // len(toks)
+        rid, pid = topo.addr(c, core)
+        trs.append(RemoteDMATransfer(dst_ids=[DstId(rid=rid, pnc=pid)], dma_engine_mask=_engines(full, k, i * k),
+                                     remote_sem=S.pin, src=T.outb[:, i * TK:(i + 1) * TK], dst=T.part[:]))
+        sent += k
+    g.remote_dma_fused(trs, local_sem=S.sent)
+    g.wait_ge(S.sent, sent)
+
+
+def rank_program(g, core, T, topo):
+    hosts, by, meet = _plan(T, topo)
+    if T.rank_of(core) is not None:
+        _rank(g, core, T, topo, hosts, by, meet)
+        return
+    for ht in hosts:
+        if meet[ht] == core:
+            _meeting(g, core, T, topo, by[ht], by[[x for x in hosts if x != ht][0]])

@@ -1,9 +1,14 @@
 from concourse.bass import DstId, RemoteDMATransfer
-from concourse.mybir import AluOpType
+from concourse.mybir import AluOpType, ActivationFunctionType
 
 TK = 32
 D = 128
 NHOSTS = 4
+TOKENS_BY_SWITCH = False
+NE_W = 8
+NE_T = 8
+NE_B = 4
+TOK_FIRST = True
 
 SCRATCH = {
     "wbuf": ("sbuf", [128, 2 * D], "bfloat16"),
@@ -41,7 +46,7 @@ def _plan(T, topo):
     meet = {}
     for ht in hosts:
         for m in range(NHOSTS):
-            if m in hosts or topo.rack(m) != topo.rack(ht):
+            if m in hosts or (topo.rack(m) == topo.rack(ht)) != TOKENS_BY_SWITCH:
                 continue
             mc = by[ht][0] + (m - ht) * topo.CORES_PER_HOST
             if all(topo.may_write(c, mc) for c in ranks) and all(topo.may_write(mc, c) for c in by[ht]):
@@ -61,21 +66,20 @@ def _compute(g, T, W, wready, X, DY, tready, n):
     pe, ve = g.tensor, g.vector
     pz, pu, pt = [T.pz0, T.pz1], [T.pu0, T.pu1], [T.pt0, T.pt1]
     pe.wait_ge(S.idn, 1)
-    for j in range(2):
-        pe.wait_ge(*wready[j])
-        pe.transpose(pt[j][:, 0:D], W[j][0], T.ident[:]).then_inc(S["tp%d" % j], 1)
     pe.wait_ge(*tready)
     for j in range(2):
+        pe.wait_ge(*wready[j])
         pe.matmul(pz[j][:, 0:n], W[j][0], X, True, True).then_inc(S["z%d" % j], 1)
         pe.matmul(pu[j][:, 0:n], W[j][1], DY, True, True).then_inc(S["u%d" % j], 1)
+        pe.transpose(pt[j][:, 0:D], W[j][0], T.ident[:]).then_inc(S["tp%d" % j], 1)
     for j in range(2):
         pe.wait_ge(S["tc%d" % j], 1)
         pe.wait_ge(S["g%d" % j], 1)
         mm = pe.matmul(T.pacc[:, 0:n], T.w1t[:, j, :], T.gb[:, j, 0:n], j == 0, j == 1)
     mm.then_inc(S.acc, 1)
     for j in range(2):
-        ve.wait_ge(S["tp%d" % j], 1)
-        ve.tensor_copy(T.w1t[:, j, :], pt[j][:, 0:D]).then_inc(S["tc%d" % j], 1)
+        g.scalar.wait_ge(S["tp%d" % j], 1)
+        g.scalar.activation(T.w1t[:, j, :], pt[j][:, 0:D], ActivationFunctionType.Copy).then_inc(S["tc%d" % j], 1)
     for j in range(2):
         ve.wait_ge(S["z%d" % j], 1)
         ve.tensor_scalar(T.mb[:, j, 0:n], pz[j][:, 0:n], 0.0, None, AluOpType.is_gt).then_inc(S["m%d" % j], 1)
@@ -92,61 +96,63 @@ def _rank(g, core, T, topo, hosts, by, meet):
     slot = by[h].index(core)
     peer = [c for c in by[h] if c != core][0]
     far, near = meet[other], meet[h]
-    g.sync.dma_start(T.wbuf[:, 0:D], T.w1[:]).then_inc(S.ldw, 16)
-    g.scalar.dma_start(T.wbuf[:, D:2 * D], T.w2t[:]).then_inc(S.ldw, 16)
-    g.sync.dma_start(T.tbuf[:, 0, :], T.x[:]).then_inc(S.ldt, 16)
-    g.scalar.dma_start(T.tbuf[:, 1, :], T.dy[:]).then_inc(S.ldt, 16)
+
+    def load_w():
+        g.sync.dma_start(T.wbuf[:, 0:D], T.w1[:]).then_inc(S.ldw, 16)
+        g.scalar.dma_start(T.wbuf[:, D:2 * D], T.w2t[:]).then_inc(S.ldw, 16)
+
+    def load_t():
+        g.sync.dma_start(T.tbuf[:, 0, :], T.x[:]).then_inc(S.ldt, 16)
+        g.scalar.dma_start(T.tbuf[:, 1, :], T.dy[:]).then_inc(S.ldt, 16)
+
+    def send_w():
+        rid, pid = topo.addr(far, core)
+        g.wait_ge(S.ldw, 32)
+        g.remote_dma(out_ap=T.lw[:, slot, :], in_ap=T.wbuf[:], remote_sem=S["wa%d" % slot], local_sem=S.sent,
+                     pid=pid, routing_id=rid, dma_engine_mask=_engines(topo.mask(core, far), NE_W))
+
+    def send_t():
+        rid, pid = topo.addr(near, core)
+        g.wait_ge(S.ldt, 32)
+        g.remote_dma(out_ap=T.lt[:, slot], in_ap=T.tbuf[:], remote_sem=S.tok, local_sem=S.sent,
+                     pid=pid, routing_id=rid, dma_engine_mask=_engines(topo.mask(core, near), NE_T))
+
+    for f in ((load_t, load_w) if TOK_FIRST else (load_w, load_t)):
+        f()
     _identity(g, T)
-    sent = 0
-    mk = topo.mask(core, far)
-    rid, pid = topo.addr(far, core)
-    g.wait_ge(S.ldw, 32)
-    g.remote_dma(out_ap=T.lw[:, slot, :], in_ap=T.wbuf[:], remote_sem=S["wa%d" % slot], local_sem=S.sent,
-                 pid=pid, routing_id=rid, dma_engine_mask=mk)
-    sent += _count(mk)
-    mk = topo.mask(core, near)
-    rid, pid = topo.addr(near, core)
-    g.wait_ge(S.ldt, 32)
-    g.remote_dma(out_ap=T.lt[:, slot], in_ap=T.tbuf[:], remote_sem=S.tok, local_sem=S.sent,
-                 pid=pid, routing_id=rid, dma_engine_mask=mk)
-    sent += _count(mk)
+    for f in ((send_t, send_w) if TOK_FIRST else (send_w, send_t)):
+        f()
     mk = topo.mask(core, peer) & ~topo.mask(core, far)
     rid, pid = topo.addr(peer, core)
     g.remote_dma(out_ap=T.lw[:, 0, :], in_ap=T.wbuf[:], remote_sem=S.wa0, local_sem=S.sent,
                  pid=pid, routing_id=rid, dma_engine_mask=mk)
     npeer = _count(mk)
-    sent += npeer
     _compute(g, T, [(T.wbuf[:, 0:D], T.wbuf[:, D:2 * D]), (T.lw[:, 0, 0:D], T.lw[:, 0, D:2 * D])],
              [(S.ldw, 32), (S.wa0, npeer)], T.tbuf[:, 0, :], T.tbuf[:, 1, :], (S.ldt, 32), TK)
-    nback = _count(topo.mask(near, core)) // len(by[h])
-    g.vector.wait_ge(S.pin, nback)
+    g.vector.wait_ge(S.pin, NE_B)
     g.vector.tensor_tensor(T.outb[:, 0:TK], T.pacc[:, 0:TK], T.part[:], AluOpType.add).then_inc(S.outr, 1)
     g.sync.wait_ge(S.outr, 1)
     g.sync.dma_start(T.dx[:], T.outb[:, 0:TK]).then_inc(S.st, 16)
     g.sync.wait_ge(S.st, 16)
-    g.wait_ge(S.sent, sent)
+    g.wait_ge(S.sent, NE_W + NE_T + npeer)
 
 
 def _meeting(g, core, T, topo, toks, wts):
     S = T.sem
     _identity(g, T)
     n = len(toks) * TK
-    nw = [_count(topo.mask(c, core)) for c in wts]
-    nt = sum(_count(topo.mask(c, core)) for c in toks)
-    _compute(g, T, [(T.lw[:, j, 0:D], T.lw[:, j, D:2 * D]) for j in range(2)], [(S.wa0, nw[0]), (S.wa1, nw[1])],
-             T.lt[:, :, 0, :], T.lt[:, :, 1, :], (S.tok, nt), n)
+    _compute(g, T, [(T.lw[:, j, 0:D], T.lw[:, j, D:2 * D]) for j in range(2)], [(S.wa0, NE_W), (S.wa1, NE_W)],
+             T.lt[:, :, 0, :], T.lt[:, :, 1, :], (S.tok, NE_T * len(toks)), n)
     g.vector.tensor_copy(T.outb[:, 0:n], T.pacc[:, 0:n]).then_inc(S.outr, 1)
     g.wait_ge(S.outr, 1)
-    trs, sent = [], 0
+    trs = []
     for i, c in enumerate(toks):
-        full = topo.mask(core, c)
-        k = _count(full) // len(toks)
         rid, pid = topo.addr(c, core)
-        trs.append(RemoteDMATransfer(dst_ids=[DstId(rid=rid, pnc=pid)], dma_engine_mask=_engines(full, k, i * k),
+        trs.append(RemoteDMATransfer(dst_ids=[DstId(rid=rid, pnc=pid)],
+                                     dma_engine_mask=_engines(topo.mask(core, c), NE_B, i * NE_B),
                                      remote_sem=S.pin, src=T.outb[:, i * TK:(i + 1) * TK], dst=T.part[:]))
-        sent += k
     g.remote_dma_fused(trs, local_sem=S.sent)
-    g.wait_ge(S.sent, sent)
+    g.wait_ge(S.sent, NE_B * len(toks))
 
 
 def rank_program(g, core, T, topo):

@@ -4,11 +4,9 @@ from concourse.mybir import AluOpType, ActivationFunctionType
 TK = 32
 D = 128
 NHOSTS = 4
-TOKENS_BY_SWITCH = False
 NE_W = 8
-NE_T = 8
+NE_T = 4
 NE_B = 4
-TOK_FIRST = True
 
 SCRATCH = {
     "wbuf": ("sbuf", [128, 2 * D], "bfloat16"),
@@ -26,8 +24,8 @@ SCRATCH = {
     "pt0": ("psum", [128, 1024], "bfloat16"), "pt1": ("psum", [128, 1024], "bfloat16"),
     "pacc": ("psum", [128, 512], "float32"),
 }
-SEMAPHORES = ["ldw", "ldt", "ones", "idn", "wa0", "wa1", "tok", "sent", "pin", "tp0", "tp1", "tc0", "tc1",
-              "z0", "z1", "u0", "u1", "m0", "m1", "g0", "g1", "acc", "outr", "st"]
+SEMAPHORES = ["ldw1", "ldw2", "ldt", "ones", "idn", "wa0", "wa1", "wb0", "wb1", "tok", "sent", "pin",
+              "tp0", "tp1", "tc0", "tc1", "z0", "z1", "u0", "u1", "m0", "m1", "g0", "g1", "acc", "outr", "st"]
 
 
 def _engines(mask, n, skip=0):
@@ -46,32 +44,27 @@ def _plan(T, topo):
     meet = {}
     for ht in hosts:
         for m in range(NHOSTS):
-            if m in hosts or (topo.rack(m) == topo.rack(ht)) != TOKENS_BY_SWITCH:
+            if m in hosts or topo.rack(m) == topo.rack(ht):
                 continue
             mc = by[ht][0] + (m - ht) * topo.CORES_PER_HOST
-            if all(topo.may_write(c, mc) for c in ranks) and all(topo.may_write(mc, c) for c in by[ht]):
+            if all(topo.may_write(c, mc) and topo.may_write(mc, c) for c in ranks):
                 meet[ht] = mc
     return hosts, by, meet
 
 
-def _identity(g, T):
-    S = T.sem
-    g.vector.memset(T.ident[:], 1.0).then_inc(S.ones, 1)
-    g.wait_ge(S.ones, 1)
-    g.affine_select(T.ident[:], T.ident[:], [[-1, D]], AluOpType.is_equal, 0.0, 0, 1).then_inc(S.idn, 1)
-
-
-def _compute(g, T, W, wready, X, DY, tready, n):
+def _compute(g, T, W, r1, r2, X, DY, tready, idready, n):
     S = T.sem
     pe, ve = g.tensor, g.vector
     pz, pu, pt = [T.pz0, T.pz1], [T.pu0, T.pu1], [T.pt0, T.pt1]
-    pe.wait_ge(S.idn, 1)
+    pe.wait_ge(*idready)
     pe.wait_ge(*tready)
     for j in range(2):
-        pe.wait_ge(*wready[j])
+        pe.wait_ge(*r1[j])
         pe.matmul(pz[j][:, 0:n], W[j][0], X, True, True).then_inc(S["z%d" % j], 1)
-        pe.matmul(pu[j][:, 0:n], W[j][1], DY, True, True).then_inc(S["u%d" % j], 1)
         pe.transpose(pt[j][:, 0:D], W[j][0], T.ident[:]).then_inc(S["tp%d" % j], 1)
+    for j in range(2):
+        pe.wait_ge(*r2[j])
+        pe.matmul(pu[j][:, 0:n], W[j][1], DY, True, True).then_inc(S["u%d" % j], 1)
     for j in range(2):
         pe.wait_ge(S["tc%d" % j], 1)
         pe.wait_ge(S["g%d" % j], 1)
@@ -83,6 +76,7 @@ def _compute(g, T, W, wready, X, DY, tready, n):
     for j in range(2):
         ve.wait_ge(S["z%d" % j], 1)
         ve.tensor_scalar(T.mb[:, j, 0:n], pz[j][:, 0:n], 0.0, None, AluOpType.is_gt).then_inc(S["m%d" % j], 1)
+    for j in range(2):
         ve.wait_ge(S["u%d" % j], 1)
         ve.wait_ge(S["m%d" % j], 1)
         ve.tensor_tensor(T.gb[:, j, 0:n], T.mb[:, j, 0:n], pu[j][:, 0:n], AluOpType.mult).then_inc(S["g%d" % j], 1)
@@ -96,63 +90,64 @@ def _rank(g, core, T, topo, hosts, by, meet):
     slot = by[h].index(core)
     peer = [c for c in by[h] if c != core][0]
     far, near = meet[other], meet[h]
-
-    def load_w():
-        g.sync.dma_start(T.wbuf[:, 0:D], T.w1[:]).then_inc(S.ldw, 16)
-        g.scalar.dma_start(T.wbuf[:, D:2 * D], T.w2t[:]).then_inc(S.ldw, 16)
-
-    def load_t():
-        g.sync.dma_start(T.tbuf[:, 0, :], T.x[:]).then_inc(S.ldt, 16)
-        g.scalar.dma_start(T.tbuf[:, 1, :], T.dy[:]).then_inc(S.ldt, 16)
-
-    def send_w():
-        rid, pid = topo.addr(far, core)
-        g.wait_ge(S.ldw, 32)
-        g.remote_dma(out_ap=T.lw[:, slot, :], in_ap=T.wbuf[:], remote_sem=S["wa%d" % slot], local_sem=S.sent,
-                     pid=pid, routing_id=rid, dma_engine_mask=_engines(topo.mask(core, far), NE_W))
-
-    def send_t():
-        rid, pid = topo.addr(near, core)
-        g.wait_ge(S.ldt, 32)
-        g.remote_dma(out_ap=T.lt[:, slot], in_ap=T.tbuf[:], remote_sem=S.tok, local_sem=S.sent,
-                     pid=pid, routing_id=rid, dma_engine_mask=_engines(topo.mask(core, near), NE_T))
-
-    for f in ((load_t, load_w) if TOK_FIRST else (load_w, load_t)):
-        f()
-    _identity(g, T)
-    for f in ((send_t, send_w) if TOK_FIRST else (send_w, send_t)):
-        f()
+    g.sync.dma_start(T.tbuf[:, 0, :], T.x[:]).then_inc(S.ldt, 16)
+    g.scalar.dma_start(T.tbuf[:, 1, :], T.dy[:]).then_inc(S.ldt, 16)
+    g.sync.dma_start(T.wbuf[:, 0:D], T.w1[:]).then_inc(S.ldw1, 16)
+    g.scalar.dma_start(T.wbuf[:, D:2 * D], T.w2t[:]).then_inc(S.ldw2, 16)
+    rid, pid = topo.addr(near, core)
+    g.wait_ge(S.ldt, 32)
+    g.remote_dma(out_ap=T.lt[:, slot], in_ap=T.tbuf[:], remote_sem=S.tok, local_sem=S.sent,
+                 pid=pid, routing_id=rid, dma_engine_mask=_engines(topo.mask(core, near), NE_T))
+    rid, pid = topo.addr(far, core)
+    mk = _engines(topo.mask(core, far), NE_W)
+    g.wait_ge(S.ldw1, 16)
+    g.remote_dma(out_ap=T.lw[:, slot, 0:D], in_ap=T.wbuf[:, 0:D], remote_sem=S["wa%d" % slot], local_sem=S.sent,
+                 pid=pid, routing_id=rid, dma_engine_mask=mk)
+    g.wait_ge(S.ldw2, 16)
+    g.remote_dma(out_ap=T.lw[:, slot, D:2 * D], in_ap=T.wbuf[:, D:2 * D], remote_sem=S["wb%d" % slot],
+                 local_sem=S.sent, pid=pid, routing_id=rid, dma_engine_mask=mk)
     mk = topo.mask(core, peer) & ~topo.mask(core, far)
     rid, pid = topo.addr(peer, core)
     g.remote_dma(out_ap=T.lw[:, 0, :], in_ap=T.wbuf[:], remote_sem=S.wa0, local_sem=S.sent,
                  pid=pid, routing_id=rid, dma_engine_mask=mk)
     npeer = _count(mk)
     _compute(g, T, [(T.wbuf[:, 0:D], T.wbuf[:, D:2 * D]), (T.lw[:, 0, 0:D], T.lw[:, 0, D:2 * D])],
-             [(S.ldw, 32), (S.wa0, npeer)], T.tbuf[:, 0, :], T.tbuf[:, 1, :], (S.ldt, 32), TK)
+             [(S.ldw1, 16), (S.wa0, npeer)], [(S.ldw2, 16), (S.wa0, npeer)],
+             T.tbuf[:, 0, :], T.tbuf[:, 1, :], (S.ldt, 32), (S.idn, NE_B), TK)
     g.vector.wait_ge(S.pin, NE_B)
     g.vector.tensor_tensor(T.outb[:, 0:TK], T.pacc[:, 0:TK], T.part[:], AluOpType.add).then_inc(S.outr, 1)
     g.sync.wait_ge(S.outr, 1)
     g.sync.dma_start(T.dx[:], T.outb[:, 0:TK]).then_inc(S.st, 16)
     g.sync.wait_ge(S.st, 16)
-    g.wait_ge(S.sent, NE_W + NE_T + npeer)
+    g.wait_ge(S.sent, NE_T + 2 * NE_W + npeer)
+
+
+def _fan(g, core, T, topo, dsts, srcs, dst_ap, sem):
+    trs = []
+    for i, c in enumerate(dsts):
+        rid, pid = topo.addr(c, core)
+        trs.append(RemoteDMATransfer(dst_ids=[DstId(rid=rid, pnc=pid)],
+                                     dma_engine_mask=_engines(topo.mask(core, c), NE_B, i * NE_B),
+                                     remote_sem=sem, src=srcs[i], dst=dst_ap))
+    g.remote_dma_fused(trs, local_sem=T.sem.sent)
+    return NE_B * len(dsts)
 
 
 def _meeting(g, core, T, topo, toks, wts):
     S = T.sem
-    _identity(g, T)
+    g.vector.memset(T.ident[:], 1.0).then_inc(S.ones, 1)
+    g.wait_ge(S.ones, 1)
+    g.affine_select(T.ident[:], T.ident[:], [[-1, D]], AluOpType.is_equal, 0.0, 0, 1).then_inc(S.idn, 1)
+    g.wait_ge(S.idn, 1)
+    sent = _fan(g, core, T, topo, wts, [T.ident[:] for c in wts], T.ident[:], S.idn)
     n = len(toks) * TK
-    _compute(g, T, [(T.lw[:, j, 0:D], T.lw[:, j, D:2 * D]) for j in range(2)], [(S.wa0, NE_W), (S.wa1, NE_W)],
-             T.lt[:, :, 0, :], T.lt[:, :, 1, :], (S.tok, NE_T * len(toks)), n)
+    _compute(g, T, [(T.lw[:, j, 0:D], T.lw[:, j, D:2 * D]) for j in range(2)],
+             [(S.wa0, NE_W), (S.wa1, NE_W)], [(S.wb0, NE_W), (S.wb1, NE_W)],
+             T.lt[:, :, 0, :], T.lt[:, :, 1, :], (S.tok, NE_T * len(toks)), (S.idn, 1), n)
     g.vector.tensor_copy(T.outb[:, 0:n], T.pacc[:, 0:n]).then_inc(S.outr, 1)
     g.wait_ge(S.outr, 1)
-    trs = []
-    for i, c in enumerate(toks):
-        rid, pid = topo.addr(c, core)
-        trs.append(RemoteDMATransfer(dst_ids=[DstId(rid=rid, pnc=pid)],
-                                     dma_engine_mask=_engines(topo.mask(core, c), NE_B, i * NE_B),
-                                     remote_sem=S.pin, src=T.outb[:, i * TK:(i + 1) * TK], dst=T.part[:]))
-    g.remote_dma_fused(trs, local_sem=S.sent)
-    g.wait_ge(S.sent, NE_B * len(toks))
+    sent += _fan(g, core, T, topo, toks, [T.outb[:, i * TK:(i + 1) * TK] for i in range(len(toks))], T.part[:], S.pin)
+    g.wait_ge(S.sent, sent)
 
 
 def rank_program(g, core, T, topo):

@@ -5,8 +5,10 @@ TK = 32
 D = 128
 NHOSTS = 4
 NE_W = 8
-NE_T = 4
+NE_T = 8
 NE_B = 4
+H = D // 2
+Q = H // 2
 
 SCRATCH = {
     "wbuf": ("sbuf", [128, 2 * D], "bfloat16"),
@@ -14,6 +16,7 @@ SCRATCH = {
     "lw": ("sbuf", [128, 2, 2 * D], "bfloat16"),
     "lt": ("sbuf", [128, 2, 2, TK], "bfloat16"),
     "part": ("sbuf", [128, TK], "bfloat16"),
+    "ramp": ("sbuf", [128, H], "bfloat16"),
     "ident": ("sbuf", [128, D], "bfloat16"),
     "w1t": ("sbuf", [128, 2, D], "bfloat16"),
     "mb": ("sbuf", [128, 2, 2 * TK], "bfloat16"),
@@ -24,8 +27,9 @@ SCRATCH = {
     "pt0": ("psum", [128, 1024], "bfloat16"), "pt1": ("psum", [128, 1024], "bfloat16"),
     "pacc": ("psum", [128, 512], "float32"),
 }
-SEMAPHORES = ["ldw1", "ldw2", "ldt", "ones", "idn", "wa0", "wa1", "wb0", "wb1", "tok", "sent", "pin",
-              "tp0", "tp1", "tc0", "tc1", "z0", "z1", "u0", "u1", "m0", "m1", "g0", "g1", "acc", "outr", "st"]
+SEMAPHORES = ["ldw1", "ldw2", "ldt", "ones", "idb", "idc", "rm1", "rm2", "idn", "wa0", "wa1", "wb0", "wb1", "tok",
+              "sent", "pin", "tp0", "tp1", "tc0", "tc1", "z0", "z1", "u0", "u1", "m0", "m1", "g0", "g1", "acc",
+              "outr", "st"]
 
 
 def _engines(mask, n, skip=0):
@@ -56,7 +60,8 @@ def _compute(g, T, W, r1, r2, X, DY, tready, idready, n):
     S = T.sem
     pe, ve = g.tensor, g.vector
     pz, pu, pt = [T.pz0, T.pz1], [T.pu0, T.pu1], [T.pt0, T.pt1]
-    pe.wait_ge(*idready)
+    for w in idready:
+        pe.wait_ge(*w)
     pe.wait_ge(*tready)
     for j in range(2):
         pe.wait_ge(*r1[j])
@@ -83,6 +88,17 @@ def _compute(g, T, W, r1, r2, X, DY, tready, idready, n):
     ve.wait_ge(S.acc, 1)
 
 
+def _quarter(g, T, q, sem):
+    g.iota(T.ramp[:, q * Q:(q + 1) * Q], [[-1, Q]], -(H + q * Q), 1,
+           allow_small_or_imprecise_dtypes=True).then_inc(sem, 1)
+
+
+def _right_half(g, T, ready):
+    for w in ready:
+        g.vector.wait_ge(*w)
+    g.vector.tensor_scalar(T.ident[:, H:D], T.ramp[:], 0.0, None, AluOpType.is_equal).then_inc(T.sem.idc, 1)
+
+
 def _rank(g, core, T, topo, hosts, by, meet):
     S = T.sem
     h = topo.host(core)
@@ -94,6 +110,12 @@ def _rank(g, core, T, topo, hosts, by, meet):
     g.scalar.dma_start(T.tbuf[:, 1, :], T.dy[:]).then_inc(S.ldt, 16)
     g.sync.dma_start(T.wbuf[:, 0:D], T.w1[:]).then_inc(S.ldw1, 16)
     g.scalar.dma_start(T.wbuf[:, D:2 * D], T.w2t[:]).then_inc(S.ldw2, 16)
+    _quarter(g, T, slot, S.rm1)
+    g.wait_ge(S.rm1, 1)
+    rid, pid = topo.addr(far, core)
+    g.remote_dma(out_ap=T.ramp[:, slot * Q:(slot + 1) * Q], in_ap=T.ramp[:, slot * Q:(slot + 1) * Q],
+                 remote_sem=S.idn, local_sem=S.sent,
+                 pid=pid, routing_id=rid, dma_engine_mask=_engines(topo.mask(core, far), NE_W))
     rid, pid = topo.addr(near, core)
     g.wait_ge(S.ldt, 32)
     g.remote_dma(out_ap=T.lt[:, slot], in_ap=T.tbuf[:], remote_sem=S.tok, local_sem=S.sent,
@@ -111,15 +133,17 @@ def _rank(g, core, T, topo, hosts, by, meet):
     g.remote_dma(out_ap=T.lw[:, 0, :], in_ap=T.wbuf[:], remote_sem=S.wa0, local_sem=S.sent,
                  pid=pid, routing_id=rid, dma_engine_mask=mk)
     npeer = _count(mk)
+    _quarter(g, T, 1 - slot, S.rm2)
+    _right_half(g, T, [(S.rm1, 1), (S.rm2, 1)])
     _compute(g, T, [(T.wbuf[:, 0:D], T.wbuf[:, D:2 * D]), (T.lw[:, 0, 0:D], T.lw[:, 0, D:2 * D])],
              [(S.ldw1, 16), (S.wa0, npeer)], [(S.ldw2, 16), (S.wa0, npeer)],
-             T.tbuf[:, 0, :], T.tbuf[:, 1, :], (S.ldt, 32), (S.idn, NE_B), TK)
+             T.tbuf[:, 0, :], T.tbuf[:, 1, :], (S.ldt, 32), [(S.idc, 1), (S.idn, NE_B)], TK)
     g.vector.wait_ge(S.pin, NE_B)
     g.vector.tensor_tensor(T.outb[:, 0:TK], T.pacc[:, 0:TK], T.part[:], AluOpType.add).then_inc(S.outr, 1)
     g.sync.wait_ge(S.outr, 1)
     g.sync.dma_start(T.dx[:], T.outb[:, 0:TK]).then_inc(S.st, 16)
     g.sync.wait_ge(S.st, 16)
-    g.wait_ge(S.sent, NE_T + 2 * NE_W + npeer)
+    g.wait_ge(S.sent, NE_T + 3 * NE_W + npeer)
 
 
 def _fan(g, core, T, topo, dsts, srcs, dst_ap, sem):
@@ -135,15 +159,16 @@ def _fan(g, core, T, topo, dsts, srcs, dst_ap, sem):
 
 def _meeting(g, core, T, topo, toks, wts):
     S = T.sem
-    g.vector.memset(T.ident[:], 1.0).then_inc(S.ones, 1)
+    g.vector.memset(T.ident[:, 0:H], 1.0).then_inc(S.ones, 1)
     g.wait_ge(S.ones, 1)
-    g.affine_select(T.ident[:], T.ident[:], [[-1, D]], AluOpType.is_equal, 0.0, 0, 1).then_inc(S.idn, 1)
-    g.wait_ge(S.idn, 1)
-    sent = _fan(g, core, T, topo, wts, [T.ident[:] for c in wts], T.ident[:], S.idn)
+    g.affine_select(T.ident[:, 0:H], T.ident[:, 0:H], [[-1, H]], AluOpType.is_equal, 0.0, 0, 1).then_inc(S.idb, 1)
+    g.wait_ge(S.idb, 1)
+    sent = _fan(g, core, T, topo, wts, [T.ident[:, 0:H] for c in wts], T.ident[:, 0:H], S.idn)
+    _right_half(g, T, [(S.idn, NE_W * len(wts))])
     n = len(toks) * TK
     _compute(g, T, [(T.lw[:, j, 0:D], T.lw[:, j, D:2 * D]) for j in range(2)],
              [(S.wa0, NE_W), (S.wa1, NE_W)], [(S.wb0, NE_W), (S.wb1, NE_W)],
-             T.lt[:, :, 0, :], T.lt[:, :, 1, :], (S.tok, NE_T * len(toks)), (S.idn, 1), n)
+             T.lt[:, :, 0, :], T.lt[:, :, 1, :], (S.tok, NE_T * len(toks)), [(S.idb, 1), (S.idc, 1)], n)
     g.vector.tensor_copy(T.outb[:, 0:n], T.pacc[:, 0:n]).then_inc(S.outr, 1)
     g.wait_ge(S.outr, 1)
     sent += _fan(g, core, T, topo, toks, [T.outb[:, i * TK:(i + 1) * TK] for i in range(len(toks))], T.part[:], S.pin)

from concourse.bass import DstId, RemoteDMATransfer
from concourse.mybir import AluOpType, ActivationFunctionType

TK = 32
D = 128
NHOSTS = 4
NE_W = 8
NE_T = 8
NE_B = 4
H = D // 2
Q = H // 2

SCRATCH = {
    "wbuf": ("sbuf", [128, 2 * D], "bfloat16"),
    "tbuf": ("sbuf", [128, 2, TK], "bfloat16"),
    "lw": ("sbuf", [128, 2, 2 * D], "bfloat16"),
    "lt": ("sbuf", [128, 2, 2, TK], "bfloat16"),
    "part": ("sbuf", [128, TK], "bfloat16"),
    "ramp": ("sbuf", [128, H], "bfloat16"),
    "ident": ("sbuf", [128, D], "bfloat16"),
    "w1t": ("sbuf", [128, 2, D], "bfloat16"),
    "mb": ("sbuf", [128, 2, 2 * TK], "bfloat16"),
    "gb": ("sbuf", [128, 2, 2 * TK], "bfloat16"),
    "outb": ("sbuf", [128, 2 * TK], "bfloat16"),
    "pz0": ("psum", [128, 512], "float32"), "pz1": ("psum", [128, 512], "float32"),
    "pu0": ("psum", [128, 512], "float32"), "pu1": ("psum", [128, 512], "float32"),
    "pt0": ("psum", [128, 1024], "bfloat16"), "pt1": ("psum", [128, 1024], "bfloat16"),
    "pacc": ("psum", [128, 512], "float32"),
}
SEMAPHORES = ["ldw1", "ldw2", "ldt", "ones", "idb", "idc", "rm1", "rm2", "idn", "wa0", "wa1", "wb0", "wb1", "tok",
              "sent", "pin", "tp0", "tp1", "tc0", "tc1", "z0", "z1", "u0", "u1", "m0", "m1", "g0", "g1", "acc",
              "outr", "st"]


def _engines(mask, n, skip=0):
    bits = [b for b in range(mask.bit_length()) if (mask >> b) & 1][skip:skip + n]
    return sum(1 << b for b in bits)


def _count(mask):
    return sum((mask >> b) & 1 for b in range(mask.bit_length()))


def _plan(T, topo):
    ranks = list(T.cores)
    hosts = sorted({topo.host(c) for c in ranks})
    by = {h: [c for c in ranks if topo.host(c) == h] for h in hosts}
    meet = {}
    for ht in hosts:
        for m in range(NHOSTS):
            if m in hosts or topo.rack(m) == topo.rack(ht):
                continue
            mc = by[ht][0] + (m - ht) * topo.CORES_PER_HOST
            if all(topo.may_write(c, mc) and topo.may_write(mc, c) for c in ranks):
                meet[ht] = mc
    return hosts, by, meet


def _compute(g, T, W, r1, r2, X, DY, tready, idready, n):
    S = T.sem
    pe, ve = g.tensor, g.vector
    pz, pu, pt = [T.pz0, T.pz1], [T.pu0, T.pu1], [T.pt0, T.pt1]
    for w in idready:
        pe.wait_ge(*w)
    pe.wait_ge(*tready)
    for j in range(2):
        pe.wait_ge(*r1[j])
        pe.matmul(pz[j][:, 0:n], W[j][0], X, True, True).then_inc(S["z%d" % j], 1)
        pe.transpose(pt[j][:, 0:D], W[j][0], T.ident[:]).then_inc(S["tp%d" % j], 1)
    for j in range(2):
        pe.wait_ge(*r2[j])
        pe.matmul(pu[j][:, 0:n], W[j][1], DY, True, True).then_inc(S["u%d" % j], 1)
    for j in range(2):
        pe.wait_ge(S["tc%d" % j], 1)
        pe.wait_ge(S["g%d" % j], 1)
        mm = pe.matmul(T.pacc[:, 0:n], T.w1t[:, j, :], T.gb[:, j, 0:n], j == 0, j == 1)
    mm.then_inc(S.acc, 1)
    for j in range(2):
        g.scalar.wait_ge(S["tp%d" % j], 1)
        g.scalar.activation(T.w1t[:, j, :], pt[j][:, 0:D], ActivationFunctionType.Copy).then_inc(S["tc%d" % j], 1)
    for j in range(2):
        ve.wait_ge(S["z%d" % j], 1)
        ve.tensor_scalar(T.mb[:, j, 0:n], pz[j][:, 0:n], 0.0, None, AluOpType.is_gt).then_inc(S["m%d" % j], 1)
    for j in range(2):
        ve.wait_ge(S["u%d" % j], 1)
        ve.wait_ge(S["m%d" % j], 1)
        ve.tensor_tensor(T.gb[:, j, 0:n], T.mb[:, j, 0:n], pu[j][:, 0:n], AluOpType.mult).then_inc(S["g%d" % j], 1)
    ve.wait_ge(S.acc, 1)


def _quarter(g, T, q, sem):
    g.iota(T.ramp[:, q * Q:(q + 1) * Q], [[-1, Q]], -(H + q * Q), 1,
           allow_small_or_imprecise_dtypes=True).then_inc(sem, 1)


def _right_half(g, T, ready):
    for w in ready:
        g.vector.wait_ge(*w)
    g.vector.tensor_scalar(T.ident[:, H:D], T.ramp[:], 0.0, None, AluOpType.is_equal).then_inc(T.sem.idc, 1)


def _rank(g, core, T, topo, hosts, by, meet):
    S = T.sem
    h = topo.host(core)
    other = [x for x in hosts if x != h][0]
    slot = by[h].index(core)
    peer = [c for c in by[h] if c != core][0]
    far, near = meet[other], meet[h]
    g.sync.dma_start(T.tbuf[:, 0, :], T.x[:]).then_inc(S.ldt, 16)
    g.scalar.dma_start(T.tbuf[:, 1, :], T.dy[:]).then_inc(S.ldt, 16)
    g.sync.dma_start(T.wbuf[:, 0:D], T.w1[:]).then_inc(S.ldw1, 16)
    g.scalar.dma_start(T.wbuf[:, D:2 * D], T.w2t[:]).then_inc(S.ldw2, 16)
    _quarter(g, T, slot, S.rm1)
    g.wait_ge(S.rm1, 1)
    rid, pid = topo.addr(far, core)
    g.remote_dma(out_ap=T.ramp[:, slot * Q:(slot + 1) * Q], in_ap=T.ramp[:, slot * Q:(slot + 1) * Q],
                 remote_sem=S.idn, local_sem=S.sent,
                 pid=pid, routing_id=rid, dma_engine_mask=_engines(topo.mask(core, far), NE_W))
    rid, pid = topo.addr(near, core)
    g.wait_ge(S.ldt, 32)
    g.remote_dma(out_ap=T.lt[:, slot], in_ap=T.tbuf[:], remote_sem=S.tok, local_sem=S.sent,
                 pid=pid, routing_id=rid, dma_engine_mask=_engines(topo.mask(core, near), NE_T))
    rid, pid = topo.addr(far, core)
    mk = _engines(topo.mask(core, far), NE_W)
    g.wait_ge(S.ldw1, 16)
    g.remote_dma(out_ap=T.lw[:, slot, 0:D], in_ap=T.wbuf[:, 0:D], remote_sem=S["wa%d" % slot], local_sem=S.sent,
                 pid=pid, routing_id=rid, dma_engine_mask=mk)
    g.wait_ge(S.ldw2, 16)
    g.remote_dma(out_ap=T.lw[:, slot, D:2 * D], in_ap=T.wbuf[:, D:2 * D], remote_sem=S["wb%d" % slot],
                 local_sem=S.sent, pid=pid, routing_id=rid, dma_engine_mask=mk)
    mk = topo.mask(core, peer) & ~topo.mask(core, far)
    rid, pid = topo.addr(peer, core)
    g.remote_dma(out_ap=T.lw[:, 0, :], in_ap=T.wbuf[:], remote_sem=S.wa0, local_sem=S.sent,
                 pid=pid, routing_id=rid, dma_engine_mask=mk)
    npeer = _count(mk)
    _quarter(g, T, 1 - slot, S.rm2)
    _right_half(g, T, [(S.rm1, 1), (S.rm2, 1)])
    _compute(g, T, [(T.wbuf[:, 0:D], T.wbuf[:, D:2 * D]), (T.lw[:, 0, 0:D], T.lw[:, 0, D:2 * D])],
             [(S.ldw1, 16), (S.wa0, npeer)], [(S.ldw2, 16), (S.wa0, npeer)],
             T.tbuf[:, 0, :], T.tbuf[:, 1, :], (S.ldt, 32), [(S.idc, 1), (S.idn, NE_B)], TK)
    g.vector.wait_ge(S.pin, NE_B)
    g.vector.tensor_tensor(T.outb[:, 0:TK], T.pacc[:, 0:TK], T.part[:], AluOpType.add).then_inc(S.outr, 1)
    g.sync.wait_ge(S.outr, 1)
    g.sync.dma_start(T.dx[:], T.outb[:, 0:TK]).then_inc(S.st, 16)
    g.sync.wait_ge(S.st, 16)
    g.wait_ge(S.sent, NE_T + 3 * NE_W + npeer)


def _fan(g, core, T, topo, dsts, srcs, dst_ap, sem):
    trs = []
    for i, c in enumerate(dsts):
        rid, pid = topo.addr(c, core)
        trs.append(RemoteDMATransfer(dst_ids=[DstId(rid=rid, pnc=pid)],
                                     dma_engine_mask=_engines(topo.mask(core, c), NE_B, i * NE_B),
                                     remote_sem=sem, src=srcs[i], dst=dst_ap))
    g.remote_dma_fused(trs, local_sem=T.sem.sent)
    return NE_B * len(dsts)


def _meeting(g, core, T, topo, toks, wts):
    S = T.sem
    g.vector.memset(T.ident[:, 0:H], 1.0).then_inc(S.ones, 1)
    g.wait_ge(S.ones, 1)
    g.affine_select(T.ident[:, 0:H], T.ident[:, 0:H], [[-1, H]], AluOpType.is_equal, 0.0, 0, 1).then_inc(S.idb, 1)
    g.wait_ge(S.idb, 1)
    sent = _fan(g, core, T, topo, wts, [T.ident[:, 0:H] for c in wts], T.ident[:, 0:H], S.idn)
    _right_half(g, T, [(S.idn, NE_W * len(wts))])
    n = len(toks) * TK
    _compute(g, T, [(T.lw[:, j, 0:D], T.lw[:, j, D:2 * D]) for j in range(2)],
             [(S.wa0, NE_W), (S.wa1, NE_W)], [(S.wb0, NE_W), (S.wb1, NE_W)],
             T.lt[:, :, 0, :], T.lt[:, :, 1, :], (S.tok, NE_T * len(toks)), [(S.idb, 1), (S.idc, 1)], n)
    g.vector.tensor_copy(T.outb[:, 0:n], T.pacc[:, 0:n]).then_inc(S.outr, 1)
    g.wait_ge(S.outr, 1)
    sent += _fan(g, core, T, topo, toks, [T.outb[:, i * TK:(i + 1) * TK] for i in range(len(toks))], T.part[:], S.pin)
    g.wait_ge(S.sent, sent)


def rank_program(g, core, T, topo):
    hosts, by, meet = _plan(T, topo)
    if T.rank_of(core) is not None:
        _rank(g, core, T, topo, hosts, by, meet)
        return
    for ht in hosts:
        if meet[ht] == core:
            _meeting(g, core, T, topo, by[ht], by[[x for x in hosts if x != ht][0]])
